import numpy as np
import ml_dtypes


def mxq(x, axis, fmt="e4m3"):
    dtype, down = {"e4m3": (ml_dtypes.float8_e4m3fn, 7), "e5m2": (ml_dtypes.float8_e5m2, 14)}[fmt]
    v = np.moveaxis(np.asarray(x, np.float32).astype(ml_dtypes.bfloat16).astype(np.float64), axis, -1)
    blocks = v.reshape(v.shape[:-1] + (-1, 32))
    amax = np.abs(blocks).max(-1, keepdims=True)
    byte = np.maximum(np.where(amax > 0, np.frexp(amax)[1] - 1 + 127, 0) - down, 1)
    scale = np.exp2(byte - 127.0)
    codes = (blocks / scale).astype(np.float32).astype(dtype).astype(np.float64)
    return np.moveaxis((codes * scale).reshape(v.shape), -1, axis)


WIDE = False


def mx_kscale(k):
    if not WIDE:
        return np.ones(k)
    levels = np.array([10, -10, 5, -5, 0])
    if k % 512:
        return np.exp2(np.random.permutation(np.resize(levels, k // 32))).repeat(32)
    a = np.empty((k // 512, 16))
    for p in range(k // 512):
        a[p, :8] = np.random.permutation(np.resize(levels, 8))
        for g in range(8):
            far = levels[np.abs(levels - a[p, g]) >= 10]
            a[p, g + 8] = far[np.random.randint(len(far))]
    return np.exp2(a.ravel()).repeat(32)


BF16 = ml_dtypes.bfloat16


def bf(x):
    return np.asarray(x, np.float32).astype(BF16)


def f64(x):
    return np.asarray(x).astype(np.float64)

E4M3FN = np.array([(-1.0 if i & 128 else 1.0) * ((1.0 + (i & 7) / 8.0) * 2.0 ** (((i >> 3) & 15) - 7) if i & 120 else (i & 7) * 2.0 ** -9) for i in range(256)])


def e4m3fn_bytes(y):
    return np.clip(np.asarray(y, np.float64), -448.0, 448.0).astype(np.float32).astype(ml_dtypes.float8_e4m3fn).view(np.uint8)


def e4m3fn_values(b):
    return E4M3FN[b]


T, K, C = 4096, 2048, 512


def setup_inputs():
    t = mx_kscale(T)
    X = 0.25 * np.random.standard_normal((T, K)) * (0.5 + np.random.random_sample((T, 1))) * t[:, None]
    X_scale = (np.max(np.abs(X), axis=1, keepdims=True) / 448.0).astype(np.float32)
    X_bytes = e4m3fn_bytes(X / f64(X_scale))
    Z = bf(2.0 * np.random.standard_normal((T, C)))
    Y = bf(np.random.random_sample((T, C)) < 0.3)
    cost = bf(4.0 * (0.5 + np.random.random_sample(T)) / np.sqrt(T) / t)
    W = bf(8.0 * np.random.standard_normal((K, C)) / np.sqrt(K))
    return {"X_bytes": X_bytes, "X_scale": X_scale, "Z": Z, "Y": Y, "cost": cost, "W": W}


def reference(X_bytes, X_scale, Z, Y, cost, W):
    X = e4m3fn_values(X_bytes) * np.repeat(f64(X_scale), K, axis=1)
    P = 1.0 / (1.0 + np.exp(-f64(Z)))
    R = (P - f64(Y)) * f64(cost)[:, None]
    D = mxq(X, 0, "e4m3").T @ mxq(R, 0, "e4m3")
    G = D + f64(W)
    return G

@@ -1,0 +1,217 @@
+from contextlib import ExitStack
+
+import concourse.mybir as mybir
+from concourse.masks import make_identity
+
+T, K, C = 4096, 2048, 512
+FLOPS = 2 * T * K * C
+
+F32 = mybir.dt.float32
+BF16 = mybir.dt.bfloat16
+U32 = mybir.dt.uint32
+U8 = mybir.dt.uint8
+FP8 = mybir.dt.float8_e4m3fn
+FP8X4 = mybir.dt.float8_e4m3fn_x4
+ACT = mybir.ActivationFunctionType
+OP = mybir.AluOpType
+
+P = 128
+G = T // 512
+CH = 128
+NCH = C // CH
+DIRECT = [4, 3, 0, 0, 0, 0, 0, 0]
+UNITS = [(0, 1024, g) for g in range(G)] + [(1024, 512, g) for g in range(G)] + [(1536, 512, g) for g in range(G)]
+NU = len(UNITS)
+
+
+def tile_logistic_weight_gradient_d3_kernel(tc, X_bytes, X_scale, Z, Y, cost, W, out):
+    nc = tc.nc
+    x_view = X_bytes.rearrange("(g p t) n -> g p t n", p=P, t=4)
+    z_view = Z.rearrange("(g p t) c -> g p t c", p=P, t=4)
+    y_view = Y.rearrange("(g p t) c -> g p t c", p=P, t=4)
+    w_view = W.rearrange("(m p) c -> p m c", p=P)
+
+    with ExitStack() as ctx:
+        const = ctx.enter_context(tc.tile_pool(name="const", bufs=1))
+        sb = ctx.enter_context(tc.tile_pool(name="sb", bufs=2))
+        ps = ctx.enter_context(tc.psum_pool(name="ps", bufs=1))
+        ctx.enter_context(tc.manual_schedule())
+
+        sc = const.tile([P, G * 4], F32, name="sc")
+        cost_b = const.tile([P, G * 4], BF16, name="cost_b")
+        cost_f = const.tile([P, G * 4], F32, name="cost_f")
+        ident = const.tile([P, P], F32, name="ident")
+        nident = const.tile([P, P], BF16, name="nident")
+        rc = const.tile([P, G, C], U32, name="rc", align_bytes=64)
+        rs = const.tile([P, G, C], U8, name="rs", align_bytes=64)
+        w_sb = const.tile([P, K // P, C], BF16, name="w_sb")
+
+        xb, zt, yt, pt, dt_, wide, il, xc, xs, rint, rbank, acc = {}, {}, {}, {}, {}, {}, {}, {}, {}, {}, {}, {}
+
+        def load_x(u):
+            c0, w, g = UNITS[u]
+            xb[u] = sb.tile([P, 4, w], U8, name="xb%d" % u, tag="xb", bufs=5)
+            nc.sync.dma_start(out=xb[u][:], in_=x_view[g][:, :, c0 : c0 + w])
+
+        def load_r(g):
+            zt[g] = sb.tile([P, 4, C], BF16, name="z%d" % g, tag="z", bufs=3)
+            nc.sync.dma_start(out=zt[g][:], in_=z_view[g])
+            yt[g] = sb.tile([P, 4, C], BF16, name="y%d" % g, tag="y", bufs=3)
+            nc.sync.dma_start(out=yt[g][:], in_=y_view[g])
+
+        def sigmoid(g):
+            pt[g] = sb.tile([P, 4, C], F32, name="p%d" % g, tag="p", bufs=2)
+            nc.scalar.activation(out=pt[g][:], in_=zt[g][:], func=ACT.Sigmoid)
+
+        def widen(u, vector=False):
+            c0, w, g = UNITS[u]
+            wide[u] = sb.tile([P, 4, w], BF16, name="wide%d" % u, tag="wide", bufs=3)
+            v = xb[u][:].bitcast(FP8)
+            for t in range(4):
+                s = sc[:, 4 * g + t : 4 * g + t + 1]
+                if vector:
+                    nc.vector.tensor_scalar(out=wide[u][:, t, :], in0=v[:, t, :], scalar1=s, scalar2=None, op0=OP.mult)
+                else:
+                    nc.scalar.activation(out=wide[u][:, t, :], in_=v[:, t, :], func=ACT.Copy, scale=s)
+
+        def interleave(u, half, halves):
+            c0, w, g = UNITS[u]
+            if half == 0:
+                il[u] = sb.tile([P, w, 4], BF16, name="il%d" % u, tag="il", bufs=2, align_bytes=64)
+            a = half * w // halves
+            b = a + w // halves
+            nc.vector.tensor_copy(
+                out=il[u][:, a:b, :].rearrange("p (c i) t -> p c t i", i=4),
+                in_=wide[u][:, :, a:b].rearrange("p t (c i) -> p c t i", i=4),
+            )
+
+        def quant_x(u):
+            c0, w, g = UNITS[u]
+            ph = "a" if w == 1024 else "b"
+            xc[u] = sb.tile([P, w], U32, name="xc%d" % u, tag="xc" + ph, bufs=8, align_bytes=64)
+            xs[u] = sb.tile([P, w], U8, name="xs%d" % u, tag="xs" + ph, bufs=8, align_bytes=64)
+            nc.vector.quantize_mx(
+                out=xc[u][:].bitcast(FP8X4), scales=xs[u][:], in_=il[u][:].rearrange("p n t -> p (n t)")
+            )
+
+        def quant_r(g):
+            nc.vector.quantize_mx(
+                out=rc[:, g, :].bitcast(FP8X4), scales=rs[:, g, :], in_=rint[g][:].rearrange("p n t -> p (n t)")
+            )
+
+        def direct_sub(g):
+            n = DIRECT[g] * CH
+            if n:
+                dt_[g] = sb.tile([P, 4, C], F32, name="d%d" % g, tag="d", bufs=1)
+                nc.vector.tensor_tensor(out=dt_[g][:, :, :n], in0=pt[g][:, :, :n], in1=yt[g][:, :, :n], op=OP.subtract)
+
+        def pe_r(g):
+            for j in range(DIRECT[g], NCH):
+                cs = slice(j * CH, (j + 1) * CH)
+                b = ps.tile([P, 4, CH], F32, name="rb%d_%d" % (g, j), tag="b%d" % j)
+                rbank[g, j] = b
+                nc.tensor.matmul(out=b[:], lhsT=ident[:], rhs=pt[g][:, :, cs], start=True, stop=False)
+                nc.tensor.matmul(out=b[:], lhsT=nident[:], rhs=yt[g][:, :, cs], start=False, stop=True)
+
+        def times_cost(g, j):
+            if j == 0:
+                rint[g] = sb.tile([P, C, 4], BF16, name="ri%d" % g, tag="ri", bufs=2, align_bytes=64)
+            cs = slice(j * CH, (j + 1) * CH)
+            src = dt_[g][:, :, cs] if j < DIRECT[g] else rbank[g, j][:]
+            nc.vector.tensor_tensor(
+                out=rint[g][:, cs, :],
+                in0=src.rearrange("p t c -> p c t"),
+                in1=cost_f[:, 4 * g : 4 * g + 4].unsqueeze(1).to_broadcast([P, CH, 4]),
+                op=OP.mult,
+            )
+
+        def mx(q, g):
+            for i in range(4):
+                m = 4 * q + i
+                if g == 0:
+                    acc[m] = ps.tile([P, C], F32, name="acc%d" % m, tag=("a%d" if q % 2 == 0 else "b%d") % i)
+                if q < 2:
+                    u, lo = g, m * P
+                else:
+                    u, lo = 8 * (q - 1) + g, i * P
+                nc.tensor.matmul_mx(
+                    out=acc[m][:],
+                    lhsT=xc[u][:, lo : lo + P].bitcast(FP8X4),
+                    lhsT_scale=xs[u][:, lo : lo + P],
+                    rhs=rc[:, g, :].bitcast(FP8X4),
+                    rhs_scale=rs[:, g, :],
+                    start=(g == 0),
+                    stop=(g == G - 1),
+                )
+
+        def add_w(m):
+            o = sb.tile([P, C], F32, name="o%d" % m, tag="o", bufs=4)
+            nc.vector.tensor_tensor(out=o[:], in0=acc[m][:], in1=w_sb[:, m, :], op=OP.add)
+            nc.sync.dma_start(out=out[m * P : (m + 1) * P, :], in_=o[:])
+
+        nc.sync.dma_start(out=sc[:].rearrange("p (g t) -> p g t", t=4), in_=X_scale.rearrange("(g p t) o -> p g (t o)", p=P, t=4))
+        load_x(0)
+        load_r(0)
+        nc.sync.dma_start(out=cost_b[:].rearrange("p (g t) -> p g t", t=4), in_=cost.rearrange("(g p t) -> p g t", p=P, t=4))
+        load_x(1)
+        load_r(1)
+        load_x(2)
+        load_r(2)
+        make_identity(nc, ident[:])
+        widen(0, vector=True)
+        nc.vector.tensor_copy(out=cost_f[:], in_=cost_b[:])
+        nc.vector.tensor_scalar(out=nident[:], in0=ident[:], scalar1=-1.0, scalar2=None, op0=OP.mult)
+        sigmoid(0)
+
+        adds = {10: [0, 1], 11: [2, 3], 14: [4, 5], 15: [6, 7], 18: [8, 9], 19: [10, 11], NU: [12, 13, 14, 15]}
+        next_q2 = 0
+        for s in range(NU + 1):
+            if s + 3 < NU:
+                load_x(s + 3)
+            if s + 3 < G:
+                load_r(s + 3)
+            if 4 <= s < 8:
+                k = s - 4
+                nc.sync.dma_start(out=w_sb[:, 4 * k : 4 * k + 4, :], in_=w_view[:, 4 * k : 4 * k + 4, :])
+            if s + 1 < G:
+                sigmoid(s + 1)
+            if s + 1 < NU:
+                widen(s + 1)
+            if s < G:
+                pe_r(s)
+            if 0 <= s - 2 < G:
+                quant_r(s - 2)
+            r = s - 1 if 0 <= s - 1 < G else None
+            halves = 2 if s < 8 else 1
+            if r is not None:
+                times_cost(r, 0)
+            if s < NU:
+                interleave(s, 0, halves)
+            if r is not None:
+                times_cost(r, 1)
+            if s >= 1:
+                quant_x(s - 1)
+            if r is not None:
+                times_cost(r, 2)
+            if s < NU and halves == 2:
+                interleave(s, 1, halves)
+            if r is not None:
+                times_cost(r, 3)
+            if s < G:
+                direct_sub(s)
+            if s < NU:
+                for m in adds.get(s, []):
+                    add_w(m)
+            if 0 <= s - 2 < G:
+                mx(0, s - 2)
+            if s == 9:
+                for g in range(G):
+                    mx(1, g)
+            if s >= 12:
+                while next_q2 < G and 9 + next_q2 <= s:
+                    mx(2, next_q2)
+                    next_q2 += 1
+            if 0 <= s - 17 < G:
+                mx(3, s - 17)
+        for m in adds[NU]:
+            add_w(m)

@@ -19,9 +19,13 @@ P = 128
 G = T // 512
 CH = 128
 NCH = C // CH
-DIRECT = [4, 3, 0, 0, 0, 0, 0, 0]
-UNITS = [(0, 1024, g) for g in range(G)] + [(1024, 512, g) for g in range(G)] + [(1536, 512, g) for g in range(G)]
+UNITS = [(0, 512, 0), (512, 512, 0)] + [(0, 1024, g) for g in range(1, G)] + [(1024, 1024, g) for g in range(6)] + [(1024, 512, 6), (1024, 512, 7), (1536, 512, 6), (1536, 256, 7), (1792, 256, 7)]
 NU = len(UNITS)
+VPL = [2, 3, 3, 3] + [0] * 16
+SIL = [128, 64] + [160] * 7 + [128] * 6 + [32, 32, 32, 64, 128]
+DIRECT = [1, 1, 2, 2, 0, 1, 0, 0]
+LEAD = 3
+ADDS = {11: [0, 1, 2, 3], 13: [4, 5, 6, 7], 18: [8, 9], 19: [10, 11]}
 
 
 def tile_logistic_weight_gradient_d3_kernel(tc, X_bytes, X_scale, Z, Y, cost, W, out):
@@ -37,25 +41,29 @@ def tile_logistic_weight_gradient_d3_kernel(tc, X_bytes, X_scale, Z, Y, cost, W,
         ps = ctx.enter_context(tc.psum_pool(name="ps", bufs=1))
         ctx.enter_context(tc.manual_schedule())
 
-        sc = const.tile([P, G * 4], F32, name="sc")
+        sc0 = const.tile([P, 4], F32, name="sc0")
+        sc = const.tile([P, (G - 1) * 4], F32, name="sc")
         cost_b = const.tile([P, G * 4], BF16, name="cost_b")
-        cost_f = const.tile([P, G * 4], F32, name="cost_f")
         ident = const.tile([P, P], F32, name="ident")
         nident = const.tile([P, P], BF16, name="nident")
         rc = const.tile([P, G, C], U32, name="rc", align_bytes=64)
         rs = const.tile([P, G, C], U8, name="rs", align_bytes=64)
         w_sb = const.tile([P, K // P, C], BF16, name="w_sb")
 
-        xb, zt, yt, pt, dt_, wide, il, xc, xs, rint, rbank, acc = {}, {}, {}, {}, {}, {}, {}, {}, {}, {}, {}, {}
+        xb, zt, yt, pt, dt_, wide, il, codes, rint, rbank, acc = {}, {}, {}, {}, {}, {}, {}, {}, {}, {}, {}
+        xcur = {}
 
-        def load_x(u):
-            c0, w, g = UNITS[u]
-            xb[u] = sb.tile([P, 4, w], U8, name="xb%d" % u, tag="xb", bufs=5)
-            nc.sync.dma_start(out=xb[u][:], in_=x_view[g][:, :, c0 : c0 + w])
+        def load_x(g, c0, w):
+            t = sb.tile([P, 4, w], U8, name="xb%d_%d" % (g, c0), tag="xb", bufs=5)
+            nc.sync.dma_start(out=t[:], in_=x_view[g][:, :, c0 : c0 + w])
+            for c in range(c0, c0 + w, 256):
+                xb[g, c] = (t, c - c0)
 
-        def load_r(g):
-            zt[g] = sb.tile([P, 4, C], BF16, name="z%d" % g, tag="z", bufs=3)
+        def load_z(g):
+            zt[g] = sb.tile([P, 4, C], BF16, name="z%d" % g, tag="z", bufs=2)
             nc.sync.dma_start(out=zt[g][:], in_=z_view[g])
+
+        def load_y(g):
             yt[g] = sb.tile([P, 4, C], BF16, name="y%d" % g, tag="y", bufs=3)
             nc.sync.dma_start(out=yt[g][:], in_=y_view[g])
 
@@ -63,36 +71,51 @@ def tile_logistic_weight_gradient_d3_kernel(tc, X_bytes, X_scale, Z, Y, cost, W,
             pt[g] = sb.tile([P, 4, C], F32, name="p%d" % g, tag="p", bufs=2)
             nc.scalar.activation(out=pt[g][:], in_=zt[g][:], func=ACT.Sigmoid)
 
-        def widen(u, vector=False):
+        def widen(u, on_vector):
             c0, w, g = UNITS[u]
-            wide[u] = sb.tile([P, 4, w], BF16, name="wide%d" % u, tag="wide", bufs=3)
-            v = xb[u][:].bitcast(FP8)
+            if u not in wide:
+                wide[u] = sb.tile([P, 4, w], BF16, name="wide%d" % u, tag="wide", bufs=3)
+            raw, lo = xb[g, c0]
+            v = raw[:].bitcast(FP8)
             for t in range(4):
-                s = sc[:, 4 * g + t : 4 * g + t + 1]
-                if vector:
-                    nc.vector.tensor_scalar(out=wide[u][:, t, :], in0=v[:, t, :], scalar1=s, scalar2=None, op0=OP.mult)
-                else:
-                    nc.scalar.activation(out=wide[u][:, t, :], in_=v[:, t, :], func=ACT.Copy, scale=s)
+                s = sc0[:, t : t + 1] if g == 0 else sc[:, 4 * g - 4 + t : 4 * g - 3 + t]
+                if t < VPL[u] and on_vector:
+                    nc.vector.tensor_scalar(out=wide[u][:, t, :], in0=v[:, t, lo : lo + w], scalar1=s, scalar2=None, op0=OP.mult)
+                if t >= VPL[u] and not on_vector:
+                    nc.scalar.activation(out=wide[u][:, t, :], in_=v[:, t, lo : lo + w], func=ACT.Copy, scale=s)
+                if t == 3 - (VPL[u] < 3) and not on_vector and u > 0:
+                    scalar_interleave(u - 1)
+
+        def il_tile(u):
+            c0, w, g = UNITS[u]
+            if u not in il:
+                il[u] = sb.tile([P, w, 4], BF16, name="il%d" % u, tag="il", bufs=3, align_bytes=64)
+            return il[u]
+
+        def scalar_interleave(u):
+            c0, w, g = UNITS[u]
+            a = w - SIL[u]
+            if a < w:
+                nc.scalar.copy(out=il_tile(u)[:, a:w, :], in_=wide[u][:, :, a:w].rearrange("p t c -> p c t"))
 
         def interleave(u, half, halves):
             c0, w, g = UNITS[u]
-            if half == 0:
-                il[u] = sb.tile([P, w, 4], BF16, name="il%d" % u, tag="il", bufs=2, align_bytes=64)
-            a = half * w // halves
-            b = a + w // halves
-            nc.vector.tensor_copy(
-                out=il[u][:, a:b, :].rearrange("p (c i) t -> p c t i", i=4),
-                in_=wide[u][:, :, a:b].rearrange("p t (c i) -> p c t i", i=4),
-            )
+            mine = w - SIL[u]
+            a = half * mine // halves
+            b = (half + 1) * mine // halves
+            if b > a:
+                nc.vector.tensor_copy(
+                    out=il_tile(u)[:, a:b, :].rearrange("p (c i) t -> p c t i", i=4),
+                    in_=wide[u][:, :, a:b].rearrange("p t (c i) -> p c t i", i=4),
+                )
 
         def quant_x(u):
             c0, w, g = UNITS[u]
-            ph = "a" if w == 1024 else "b"
-            xc[u] = sb.tile([P, w], U32, name="xc%d" % u, tag="xc" + ph, bufs=8, align_bytes=64)
-            xs[u] = sb.tile([P, w], U8, name="xs%d" % u, tag="xs" + ph, bufs=8, align_bytes=64)
-            nc.vector.quantize_mx(
-                out=xc[u][:].bitcast(FP8X4), scales=xs[u][:], in_=il[u][:].rearrange("p n t -> p (n t)")
-            )
+            xc = sb.tile([P, w], U32, name="xc%d" % u, tag="xc", bufs=12, align_bytes=64)
+            xs = sb.tile([P, w], U8, name="xs%d" % u, tag="xs", bufs=12, align_bytes=64)
+            nc.vector.quantize_mx(out=xc[:].bitcast(FP8X4), scales=xs[:], in_=il[u][:].rearrange("p n t -> p (n t)"))
+            for lo in range(0, w, P):
+                codes[(c0 + lo) // P, g] = (xc, xs, lo)
 
         def quant_r(g):
             nc.vector.quantize_mx(
@@ -102,8 +125,8 @@ def tile_logistic_weight_gradient_d3_kernel(tc, X_bytes, X_scale, Z, Y, cost, W,
         def direct_sub(g):
             n = DIRECT[g] * CH
             if n:
-                dt_[g] = sb.tile([P, 4, C], F32, name="d%d" % g, tag="d", bufs=1)
-                nc.vector.tensor_tensor(out=dt_[g][:, :, :n], in0=pt[g][:, :, :n], in1=yt[g][:, :, :n], op=OP.subtract)
+                dt_[g] = sb.tile([P, 4, n], F32, name="d%d" % g, tag="d", bufs=1)
+                nc.vector.tensor_tensor(out=dt_[g][:], in0=pt[g][:, :, :n], in1=yt[g][:, :, :n], op=OP.subtract)
 
         def pe_r(g):
             for j in range(DIRECT[g], NCH):
@@ -121,74 +144,91 @@ def tile_logistic_weight_gradient_d3_kernel(tc, X_bytes, X_scale, Z, Y, cost, W,
             nc.vector.tensor_tensor(
                 out=rint[g][:, cs, :],
                 in0=src.rearrange("p t c -> p c t"),
-                in1=cost_f[:, 4 * g : 4 * g + 4].unsqueeze(1).to_broadcast([P, CH, 4]),
+                in1=cost_b[:, 4 * g : 4 * g + 4].unsqueeze(1).to_broadcast([P, CH, 4]),
                 op=OP.mult,
             )
 
-        def mx(q, g):
-            for i in range(4):
-                m = 4 * q + i
-                if g == 0:
-                    acc[m] = ps.tile([P, C], F32, name="acc%d" % m, tag=("a%d" if q % 2 == 0 else "b%d") % i)
-                if q < 2:
-                    u, lo = g, m * P
-                else:
-                    u, lo = 8 * (q - 1) + g, i * P
-                nc.tensor.matmul_mx(
-                    out=acc[m][:],
-                    lhsT=xc[u][:, lo : lo + P].bitcast(FP8X4),
-                    lhsT_scale=xs[u][:, lo : lo + P],
-                    rhs=rc[:, g, :].bitcast(FP8X4),
-                    rhs_scale=rs[:, g, :],
-                    start=(g == 0),
-                    stop=(g == G - 1),
-                )
+        def mx(m, g):
+            if g == 0:
+                acc[m] = ps.tile([P, C], F32, name="acc%d" % m, tag=("a%d" if (m // 4) % 2 == 0 else "b%d") % (m % 4))
+            xc, xs, lo = codes[m, g]
+            nc.tensor.matmul_mx(
+                out=acc[m][:],
+                lhsT=xc[:, lo : lo + P].bitcast(FP8X4),
+                lhsT_scale=xs[:, lo : lo + P],
+                rhs=rc[:, g, :].bitcast(FP8X4),
+                rhs_scale=rs[:, g, :],
+                start=(g == 0),
+                stop=(g == G - 1),
+            )
 
         def add_w(m):
-            o = sb.tile([P, C], F32, name="o%d" % m, tag="o", bufs=4)
+            o = sb.tile([P, C], F32, name="o%d" % m, tag="o", bufs=6)
             nc.vector.tensor_tensor(out=o[:], in0=acc[m][:], in1=w_sb[:, m, :], op=OP.add)
             nc.sync.dma_start(out=out[m * P : (m + 1) * P, :], in_=o[:])
 
-        nc.sync.dma_start(out=sc[:].rearrange("p (g t) -> p g t", t=4), in_=X_scale.rearrange("(g p t) o -> p g (t o)", p=P, t=4))
-        load_x(0)
-        load_r(0)
-        nc.sync.dma_start(out=cost_b[:].rearrange("p (g t) -> p g t", t=4), in_=cost.rearrange("(g p t) -> p g t", p=P, t=4))
-        load_x(1)
-        load_r(1)
-        load_x(2)
-        load_r(2)
-        make_identity(nc, ident[:])
-        widen(0, vector=True)
-        nc.vector.tensor_copy(out=cost_f[:], in_=cost_b[:])
-        nc.vector.tensor_scalar(out=nident[:], in0=ident[:], scalar1=-1.0, scalar2=None, op0=OP.mult)
-        sigmoid(0)
+        nc.scalar.dma_start(out=sc0[:], in_=X_scale[:512, :].rearrange("(p t) o -> p (t o)", t=4))
+        nc.scalar.dma_start(
+            out=sc[:].rearrange("p (g t) -> p g t", t=4),
+            in_=X_scale[512:, :].rearrange("(g p t) o -> p g (t o)", p=P, t=4),
+        )
+        load_x(0, 0, 512)
+        load_x(0, 512, 512)
+        load_z(0)
+        nc.scalar.dma_start(out=cost_b[:].rearrange("p (g t) -> p g t", t=4), in_=cost.rearrange("(g p t) -> p g t", p=P, t=4))
+        load_y(0)
+        pending = []
+        for g in range(1, G):
+            pending += [("x", g, 0, 1024, g), ("z", g, 0, 0, g - 1), ("y", g, 0, 0, g)]
+        pending += [("x", 0, 1024, 1024, 9), ("x", 1, 1024, 1024, 10)]
+        for k in range(4):
+            pending += [("w", k, 0, 0, 10), ("x", 2 + k, 1024, 1024, 11 + k)]
+        pending += [("x", 6, 1024, 512, 15), ("x", 7, 1024, 512, 16), ("x", 6, 1536, 512, 17), ("x", 7, 1536, 512, 18)]
 
-        adds = {10: [0, 1], 11: [2, 3], 14: [4, 5], 15: [6, 7], 18: [8, 9], 19: [10, 11], NU: [12, 13, 14, 15]}
-        next_q2 = 0
+        def load_until(step):
+            while pending and pending[0][4] <= step:
+                kind, g, c0, w, need = pending.pop(0)
+                if kind == "x":
+                    load_x(g, c0, w)
+                if kind == "z":
+                    load_z(g)
+                if kind == "y":
+                    load_y(g)
+                if kind == "w":
+                    nc.sync.dma_start(out=w_sb[:, 4 * g : 4 * g + 4, :], in_=w_view[:, 4 * g : 4 * g + 4, :])
+
+        load_until(LEAD - 1)
+        make_identity(nc, ident[:])
+        widen(0, True)
+        widen(0, False)
+        nc.vector.tensor_scalar(out=nident[:], in0=ident[:], scalar1=-1.0, scalar2=None, op0=OP.mult)
+
+        next_g = [0] * 16
+        added = set()
         for s in range(NU + 1):
-            if s + 3 < NU:
-                load_x(s + 3)
-            if s + 3 < G:
-                load_r(s + 3)
-            if 4 <= s < 8:
-                k = s - 4
-                nc.sync.dma_start(out=w_sb[:, 4 * k : 4 * k + 4, :], in_=w_view[:, 4 * k : 4 * k + 4, :])
-            if s + 1 < G:
-                sigmoid(s + 1)
+            load_until(s + LEAD)
             if s + 1 < NU:
-                widen(s + 1)
+                widen(s + 1, True)
             if s < G:
-                pe_r(s)
-            if 0 <= s - 2 < G:
-                quant_r(s - 2)
-            r = s - 1 if 0 <= s - 1 < G else None
-            halves = 2 if s < 8 else 1
+                sigmoid(s)
+            if s + 1 < NU:
+                widen(s + 1, False)
+            elif s < NU:
+                scalar_interleave(s)
+            if 0 <= s - 1 < G:
+                pe_r(s - 1)
+            r = s - 2 if 0 <= s - 2 < G else None
+            halves = 2 if r is not None else 1
             if r is not None:
                 times_cost(r, 0)
+            if 0 <= s - 3 < G:
+                quant_r(s - 3)
             if s < NU:
                 interleave(s, 0, halves)
             if r is not None:
                 times_cost(r, 1)
+            if 0 <= s - 1 < G:
+                direct_sub(s - 1)
             if s >= 1:
                 quant_x(s - 1)
             if r is not None:
@@ -197,21 +237,12 @@ def tile_logistic_weight_gradient_d3_kernel(tc, X_bytes, X_scale, Z, Y, cost, W,
                 interleave(s, 1, halves)
             if r is not None:
                 times_cost(r, 3)
-            if s < G:
-                direct_sub(s)
-            if s < NU:
-                for m in adds.get(s, []):
-                    add_w(m)
-            if 0 <= s - 2 < G:
-                mx(0, s - 2)
-            if s == 9:
-                for g in range(G):
-                    mx(1, g)
-            if s >= 12:
-                while next_q2 < G and 9 + next_q2 <= s:
-                    mx(2, next_q2)
-                    next_q2 += 1
-            if 0 <= s - 17 < G:
-                mx(3, s - 17)
-        for m in adds[NU]:
+            for m in ADDS.get(s, []):
+                add_w(m)
+                added.add(m)
+            for m in range(16):
+                while next_g[m] < G and (m, next_g[m]) in codes and next_g[m] <= s - 3 and (m < 4 or (m < 8 and s >= 10) or m - 8 in added):
+                    mx(m, next_g[m])
+                    next_g[m] += 1
+        for m in (12, 13, 14, 15):
             add_w(m)

@@ -21,11 +21,11 @@ CH = 128
 NCH = C // CH
 UNITS = [(0, 512, 0), (512, 512, 0)] + [(0, 1024, g) for g in range(1, G)] + [(1024, 1024, g) for g in range(6)] + [(1024, 512, 6), (1024, 512, 7), (1536, 512, 6), (1536, 256, 7), (1792, 256, 7)]
 NU = len(UNITS)
-VPL = [2, 3, 3, 3] + [0] * 16
-SIL = [128, 64] + [160] * 7 + [128] * 6 + [32, 32, 32, 64, 128]
-DIRECT = [1, 1, 2, 2, 0, 1, 0, 0]
-LEAD = 3
-ADDS = {11: [0, 1, 2, 3], 13: [4, 5, 6, 7], 18: [8, 9], 19: [10, 11]}
+VPL = [3, 1, 3, 3, 1, 1] + [0] * 14
+SIL = [128, 128, 128, 0, 0] + [128] * 10 + [128, 128, 64, 128, 256]
+DIRECT = [1, 1, 1, 1, 1, 1, 1, 0]
+RD, LEAD, ZB, YB, XB, CB = 1, 4, 3, 4, 6, 12
+ADDS = {12: [0, 1, 2, 3], 13: [4, 5, 6], 14: [7], 19: [8, 9, 10, 11]}
 
 
 def tile_logistic_weight_gradient_d3_kernel(tc, X_bytes, X_scale, Z, Y, cost, W, out):
@@ -54,17 +54,17 @@ def tile_logistic_weight_gradient_d3_kernel(tc, X_bytes, X_scale, Z, Y, cost, W,
         xcur = {}
 
         def load_x(g, c0, w):
-            t = sb.tile([P, 4, w], U8, name="xb%d_%d" % (g, c0), tag="xb", bufs=5)
+            t = sb.tile([P, 4, w], U8, name="xb%d_%d" % (g, c0), tag="xb", bufs=XB)
             nc.sync.dma_start(out=t[:], in_=x_view[g][:, :, c0 : c0 + w])
             for c in range(c0, c0 + w, 256):
                 xb[g, c] = (t, c - c0)
 
         def load_z(g):
-            zt[g] = sb.tile([P, 4, C], BF16, name="z%d" % g, tag="z", bufs=2)
+            zt[g] = sb.tile([P, 4, C], BF16, name="z%d" % g, tag="z", bufs=ZB)
             nc.sync.dma_start(out=zt[g][:], in_=z_view[g])
 
         def load_y(g):
-            yt[g] = sb.tile([P, 4, C], BF16, name="y%d" % g, tag="y", bufs=3)
+            yt[g] = sb.tile([P, 4, C], BF16, name="y%d" % g, tag="y", bufs=YB)
             nc.sync.dma_start(out=yt[g][:], in_=y_view[g])
 
         def sigmoid(g):
@@ -111,8 +111,8 @@ def tile_logistic_weight_gradient_d3_kernel(tc, X_bytes, X_scale, Z, Y, cost, W,
 
         def quant_x(u):
             c0, w, g = UNITS[u]
-            xc = sb.tile([P, w], U32, name="xc%d" % u, tag="xc", bufs=12, align_bytes=64)
-            xs = sb.tile([P, w], U8, name="xs%d" % u, tag="xs", bufs=12, align_bytes=64)
+            xc = sb.tile([P, w], U32, name="xc%d" % u, tag="xc", bufs=CB, align_bytes=64)
+            xs = sb.tile([P, w], U8, name="xs%d" % u, tag="xs", bufs=CB, align_bytes=64)
             nc.vector.quantize_mx(out=xc[:].bitcast(FP8X4), scales=xs[:], in_=il[u][:].rearrange("p n t -> p (n t)"))
             for lo in range(0, w, P):
                 codes[(c0 + lo) // P, g] = (xc, xs, lo)
@@ -174,12 +174,13 @@ def tile_logistic_weight_gradient_d3_kernel(tc, X_bytes, X_scale, Z, Y, cost, W,
         )
         load_x(0, 0, 512)
         load_x(0, 512, 512)
-        load_z(0)
         nc.scalar.dma_start(out=cost_b[:].rearrange("p (g t) -> p g t", t=4), in_=cost.rearrange("(g p t) -> p g t", p=P, t=4))
-        load_y(0)
-        pending = []
-        for g in range(1, G):
-            pending += [("x", g, 0, 1024, g), ("z", g, 0, 0, g - 1), ("y", g, 0, 0, g)]
+        pending = [("x", 1, 0, 1024, 1)]
+        for g in range(G):
+            pending += [("z", g, 0, 0, g + RD - 1)]
+            if g + 2 < G:
+                pending += [("x", g + 2, 0, 1024, g + 2)]
+            pending += [("y", g, 0, 0, g + RD)]
         pending += [("x", 0, 1024, 1024, 9), ("x", 1, 1024, 1024, 10)]
         for k in range(4):
             pending += [("w", k, 0, 0, 10), ("x", 2 + k, 1024, 1024, 11 + k)]
@@ -209,26 +210,26 @@ def tile_logistic_weight_gradient_d3_kernel(tc, X_bytes, X_scale, Z, Y, cost, W,
             load_until(s + LEAD)
             if s + 1 < NU:
                 widen(s + 1, True)
-            if s < G:
-                sigmoid(s)
+            if 0 <= s - RD < G:
+                sigmoid(s - RD)
             if s + 1 < NU:
                 widen(s + 1, False)
             elif s < NU:
                 scalar_interleave(s)
-            if 0 <= s - 1 < G:
-                pe_r(s - 1)
-            r = s - 2 if 0 <= s - 2 < G else None
+            if 0 <= s - RD - 1 < G:
+                pe_r(s - RD - 1)
+            r = s - RD - 2 if 0 <= s - RD - 2 < G else None
             halves = 2 if r is not None else 1
             if r is not None:
                 times_cost(r, 0)
-            if 0 <= s - 3 < G:
-                quant_r(s - 3)
+            if 0 <= s - RD - 3 < G:
+                quant_r(s - RD - 3)
             if s < NU:
                 interleave(s, 0, halves)
             if r is not None:
                 times_cost(r, 1)
-            if 0 <= s - 1 < G:
-                direct_sub(s - 1)
+            if 0 <= s - RD - 1 < G:
+                direct_sub(s - RD - 1)
             if s >= 1:
                 quant_x(s - 1)
             if r is not None:
@@ -241,7 +242,7 @@ def tile_logistic_weight_gradient_d3_kernel(tc, X_bytes, X_scale, Z, Y, cost, W,
                 add_w(m)
                 added.add(m)
             for m in range(16):
-                while next_g[m] < G and (m, next_g[m]) in codes and next_g[m] <= s - 3 and (m < 4 or (m < 8 and s >= 10) or m - 8 in added):
+                while next_g[m] < G and (m, next_g[m]) in codes and next_g[m] <= s - RD - 3 and (m < 4 or (m < 8 and s >= 10 + RD) or m - 8 in added):
                     mx(m, next_g[m])
                     next_g[m] += 1
         for m in (12, 13, 14, 15):

@@ -96,7 +96,10 @@ def tile_logistic_weight_gradient_d3_kernel(tc, X_bytes, X_scale, Z, Y, cost, W,
             c0, w, g = UNITS[u]
             a = w - SIL[u]
             if a < w:
-                nc.scalar.copy(out=il_tile(u)[:, a:w, :], in_=wide[u][:, :, a:w].rearrange("p t c -> p c t"))
+                nc.scalar.copy(
+                    out=il_tile(u)[:, a:w, :].rearrange("p (c i) t -> p c t i", i=4),
+                    in_=wide[u][:, :, a:w].rearrange("p t (c i) -> p c t i", i=4),
+                )
 
         def interleave(u, half, halves):
             c0, w, g = UNITS[u]

@@ -21,11 +21,11 @@ CH = 128
 NCH = C // CH
 UNITS = [(0, 512, 0), (512, 512, 0)] + [(0, 1024, g) for g in range(1, G)] + [(1024, 1024, g) for g in range(6)] + [(1024, 512, 6), (1024, 512, 7), (1536, 512, 6), (1536, 256, 7), (1792, 256, 7)]
 NU = len(UNITS)
-VPL = [3, 1, 3, 3, 1, 1] + [0] * 14
-SIL = [128, 128, 128, 0, 0] + [128] * 10 + [128, 128, 64, 128, 256]
+VPL = [3, 0, 4, 2, 1] + [0] * 15
+SIL = [64, 64] + [0] * 6 + [96] * 7 + [0, 0, 128, 160, 256]
 DIRECT = [1, 1, 1, 1, 1, 1, 1, 0]
 RD, LEAD, ZB, YB, XB, CB = 1, 4, 3, 4, 6, 12
-ADDS = {12: [0, 1, 2, 3], 13: [4, 5, 6], 14: [7], 19: [8, 9, 10, 11]}
+ADDS = {12: [0, 1, 2, 3], 13: [4, 5, 6, 7], 19: [8, 9, 10, 11]}
 
 
 def tile_logistic_weight_gradient_d3_kernel(tc, X_bytes, X_scale, Z, Y, cost, W, out):

from contextlib import ExitStack

import concourse.mybir as mybir
from concourse.masks import make_identity

T, K, C = 4096, 2048, 512
FLOPS = 2 * T * K * C

F32 = mybir.dt.float32
BF16 = mybir.dt.bfloat16
U32 = mybir.dt.uint32
U8 = mybir.dt.uint8
FP8 = mybir.dt.float8_e4m3fn
FP8X4 = mybir.dt.float8_e4m3fn_x4
ACT = mybir.ActivationFunctionType
OP = mybir.AluOpType

P = 128
G = T // 512
CH = 128
NCH = C // CH
UNITS = [(0, 512, 0), (512, 512, 0)] + [(0, 1024, g) for g in range(1, G)] + [(1024, 1024, g) for g in range(6)] + [(1024, 512, 6), (1024, 512, 7), (1536, 512, 6), (1536, 256, 7), (1792, 256, 7)]
NU = len(UNITS)
VPL = [3, 0, 4, 2, 1] + [0] * 15
SIL = [64, 64] + [0] * 6 + [96] * 7 + [0, 0, 128, 160, 256]
DIRECT = [1, 1, 1, 1, 1, 1, 1, 0]
RD, LEAD, ZB, YB, XB, CB = 1, 4, 3, 4, 6, 12
ADDS = {12: [0, 1, 2, 3], 13: [4, 5, 6, 7], 19: [8, 9, 10, 11]}


def tile_logistic_weight_gradient_d3_kernel(tc, X_bytes, X_scale, Z, Y, cost, W, out):
    nc = tc.nc
    x_view = X_bytes.rearrange("(g p t) n -> g p t n", p=P, t=4)
    z_view = Z.rearrange("(g p t) c -> g p t c", p=P, t=4)
    y_view = Y.rearrange("(g p t) c -> g p t c", p=P, t=4)
    w_view = W.rearrange("(m p) c -> p m c", p=P)

    with ExitStack() as ctx:
        const = ctx.enter_context(tc.tile_pool(name="const", bufs=1))
        sb = ctx.enter_context(tc.tile_pool(name="sb", bufs=2))
        ps = ctx.enter_context(tc.psum_pool(name="ps", bufs=1))
        ctx.enter_context(tc.manual_schedule())

        sc0 = const.tile([P, 4], F32, name="sc0")
        sc = const.tile([P, (G - 1) * 4], F32, name="sc")
        cost_b = const.tile([P, G * 4], BF16, name="cost_b")
        ident = const.tile([P, P], F32, name="ident")
        nident = const.tile([P, P], BF16, name="nident")
        rc = const.tile([P, G, C], U32, name="rc", align_bytes=64)
        rs = const.tile([P, G, C], U8, name="rs", align_bytes=64)
        w_sb = const.tile([P, K // P, C], BF16, name="w_sb")

        xb, zt, yt, pt, dt_, wide, il, codes, rint, rbank, acc = {}, {}, {}, {}, {}, {}, {}, {}, {}, {}, {}
        xcur = {}

        def load_x(g, c0, w):
            t = sb.tile([P, 4, w], U8, name="xb%d_%d" % (g, c0), tag="xb", bufs=XB)
            nc.sync.dma_start(out=t[:], in_=x_view[g][:, :, c0 : c0 + w])
            for c in range(c0, c0 + w, 256):
                xb[g, c] = (t, c - c0)

        def load_z(g):
            zt[g] = sb.tile([P, 4, C], BF16, name="z%d" % g, tag="z", bufs=ZB)
            nc.sync.dma_start(out=zt[g][:], in_=z_view[g])

        def load_y(g):
            yt[g] = sb.tile([P, 4, C], BF16, name="y%d" % g, tag="y", bufs=YB)
            nc.sync.dma_start(out=yt[g][:], in_=y_view[g])

        def sigmoid(g):
            pt[g] = sb.tile([P, 4, C], F32, name="p%d" % g, tag="p", bufs=2)
            nc.scalar.activation(out=pt[g][:], in_=zt[g][:], func=ACT.Sigmoid)

        def widen(u, on_vector):
            c0, w, g = UNITS[u]
            if u not in wide:
                wide[u] = sb.tile([P, 4, w], BF16, name="wide%d" % u, tag="wide", bufs=3)
            raw, lo = xb[g, c0]
            v = raw[:].bitcast(FP8)
            for t in range(4):
                s = sc0[:, t : t + 1] if g == 0 else sc[:, 4 * g - 4 + t : 4 * g - 3 + t]
                if t < VPL[u] and on_vector:
                    nc.vector.tensor_scalar(out=wide[u][:, t, :], in0=v[:, t, lo : lo + w], scalar1=s, scalar2=None, op0=OP.mult)
                if t >= VPL[u] and not on_vector:
                    nc.scalar.activation(out=wide[u][:, t, :], in_=v[:, t, lo : lo + w], func=ACT.Copy, scale=s)
                if t == 3 - (VPL[u] < 3) and not on_vector and u > 0:
                    scalar_interleave(u - 1)

        def il_tile(u):
            c0, w, g = UNITS[u]
            if u not in il:
                il[u] = sb.tile([P, w, 4], BF16, name="il%d" % u, tag="il", bufs=3, align_bytes=64)
            return il[u]

        def scalar_interleave(u):
            c0, w, g = UNITS[u]
            a = w - SIL[u]
            if a < w:
                nc.scalar.copy(
                    out=il_tile(u)[:, a:w, :].rearrange("p (c i) t -> p c t i", i=4),
                    in_=wide[u][:, :, a:w].rearrange("p t (c i) -> p c t i", i=4),
                )

        def interleave(u, half, halves):
            c0, w, g = UNITS[u]
            mine = w - SIL[u]
            a = half * mine // halves
            b = (half + 1) * mine // halves
            if b > a:
                nc.vector.tensor_copy(
                    out=il_tile(u)[:, a:b, :].rearrange("p (c i) t -> p c t i", i=4),
                    in_=wide[u][:, :, a:b].rearrange("p t (c i) -> p c t i", i=4),
                )

        def quant_x(u):
            c0, w, g = UNITS[u]
            xc = sb.tile([P, w], U32, name="xc%d" % u, tag="xc", bufs=CB, align_bytes=64)
            xs = sb.tile([P, w], U8, name="xs%d" % u, tag="xs", bufs=CB, align_bytes=64)
            nc.vector.quantize_mx(out=xc[:].bitcast(FP8X4), scales=xs[:], in_=il[u][:].rearrange("p n t -> p (n t)"))
            for lo in range(0, w, P):
                codes[(c0 + lo) // P, g] = (xc, xs, lo)

        def quant_r(g):
            nc.vector.quantize_mx(
                out=rc[:, g, :].bitcast(FP8X4), scales=rs[:, g, :], in_=rint[g][:].rearrange("p n t -> p (n t)")
            )

        def direct_sub(g):
            n = DIRECT[g] * CH
            if n:
                dt_[g] = sb.tile([P, 4, n], F32, name="d%d" % g, tag="d", bufs=1)
                nc.vector.tensor_tensor(out=dt_[g][:], in0=pt[g][:, :, :n], in1=yt[g][:, :, :n], op=OP.subtract)

        def pe_r(g):
            for j in range(DIRECT[g], NCH):
                cs = slice(j * CH, (j + 1) * CH)
                b = ps.tile([P, 4, CH], F32, name="rb%d_%d" % (g, j), tag="b%d" % j)
                rbank[g, j] = b
                nc.tensor.matmul(out=b[:], lhsT=ident[:], rhs=pt[g][:, :, cs], start=True, stop=False)
                nc.tensor.matmul(out=b[:], lhsT=nident[:], rhs=yt[g][:, :, cs], start=False, stop=True)

        def times_cost(g, j):
            if j == 0:
                rint[g] = sb.tile([P, C, 4], BF16, name="ri%d" % g, tag="ri", bufs=2, align_bytes=64)
            cs = slice(j * CH, (j + 1) * CH)
            src = dt_[g][:, :, cs] if j < DIRECT[g] else rbank[g, j][:]
            nc.vector.tensor_tensor(
                out=rint[g][:, cs, :],
                in0=src.rearrange("p t c -> p c t"),
                in1=cost_b[:, 4 * g : 4 * g + 4].unsqueeze(1).to_broadcast([P, CH, 4]),
                op=OP.mult,
            )

        def mx(m, g):
            if g == 0:
                acc[m] = ps.tile([P, C], F32, name="acc%d" % m, tag=("a%d" if (m // 4) % 2 == 0 else "b%d") % (m % 4))
            xc, xs, lo = codes[m, g]
            nc.tensor.matmul_mx(
                out=acc[m][:],
                lhsT=xc[:, lo : lo + P].bitcast(FP8X4),
                lhsT_scale=xs[:, lo : lo + P],
                rhs=rc[:, g, :].bitcast(FP8X4),
                rhs_scale=rs[:, g, :],
                start=(g == 0),
                stop=(g == G - 1),
            )

        def add_w(m):
            o = sb.tile([P, C], F32, name="o%d" % m, tag="o", bufs=6)
            nc.vector.tensor_tensor(out=o[:], in0=acc[m][:], in1=w_sb[:, m, :], op=OP.add)
            nc.sync.dma_start(out=out[m * P : (m + 1) * P, :], in_=o[:])

        nc.scalar.dma_start(out=sc0[:], in_=X_scale[:512, :].rearrange("(p t) o -> p (t o)", t=4))
        nc.scalar.dma_start(
            out=sc[:].rearrange("p (g t) -> p g t", t=4),
            in_=X_scale[512:, :].rearrange("(g p t) o -> p g (t o)", p=P, t=4),
        )
        load_x(0, 0, 512)
        load_x(0, 512, 512)
        nc.scalar.dma_start(out=cost_b[:].rearrange("p (g t) -> p g t", t=4), in_=cost.rearrange("(g p t) -> p g t", p=P, t=4))
        pending = [("x", 1, 0, 1024, 1)]
        for g in range(G):
            pending += [("z", g, 0, 0, g + RD - 1)]
            if g + 2 < G:
                pending += [("x", g + 2, 0, 1024, g + 2)]
            pending += [("y", g, 0, 0, g + RD)]
        pending += [("x", 0, 1024, 1024, 9), ("x", 1, 1024, 1024, 10)]
        for k in range(4):
            pending += [("w", k, 0, 0, 10), ("x", 2 + k, 1024, 1024, 11 + k)]
        pending += [("x", 6, 1024, 512, 15), ("x", 7, 1024, 512, 16), ("x", 6, 1536, 512, 17), ("x", 7, 1536, 512, 18)]

        def load_until(step):
            while pending and pending[0][4] <= step:
                kind, g, c0, w, need = pending.pop(0)
                if kind == "x":
                    load_x(g, c0, w)
                if kind == "z":
                    load_z(g)
                if kind == "y":
                    load_y(g)
                if kind == "w":
                    nc.sync.dma_start(out=w_sb[:, 4 * g : 4 * g + 4, :], in_=w_view[:, 4 * g : 4 * g + 4, :])

        load_until(LEAD - 1)
        make_identity(nc, ident[:])
        widen(0, True)
        widen(0, False)
        nc.vector.tensor_scalar(out=nident[:], in0=ident[:], scalar1=-1.0, scalar2=None, op0=OP.mult)

        next_g = [0] * 16
        added = set()
        for s in range(NU + 1):
            load_until(s + LEAD)
            if s + 1 < NU:
                widen(s + 1, True)
            if 0 <= s - RD < G:
                sigmoid(s - RD)
            if s + 1 < NU:
                widen(s + 1, False)
            elif s < NU:
                scalar_interleave(s)
            if 0 <= s - RD - 1 < G:
                pe_r(s - RD - 1)
            r = s - RD - 2 if 0 <= s - RD - 2 < G else None
            halves = 2 if r is not None else 1
            if r is not None:
                times_cost(r, 0)
            if 0 <= s - RD - 3 < G:
                quant_r(s - RD - 3)
            if s < NU:
                interleave(s, 0, halves)
            if r is not None:
                times_cost(r, 1)
            if 0 <= s - RD - 1 < G:
                direct_sub(s - RD - 1)
            if s >= 1:
                quant_x(s - 1)
            if r is not None:
                times_cost(r, 2)
            if s < NU and halves == 2:
                interleave(s, 1, halves)
            if r is not None:
                times_cost(r, 3)
            for m in ADDS.get(s, []):
                add_w(m)
                added.add(m)
            for m in range(16):
                while next_g[m] < G and (m, next_g[m]) in codes and next_g[m] <= s - RD - 3 and (m < 4 or (m < 8 and s >= 10 + RD) or m - 8 in added):
                    mx(m, next_g[m])
                    next_g[m] += 1
        for m in (12, 13, 14, 15):
            add_w(m)
